import numpy as np
import ml_dtypes


def mxq(x, axis, fmt="e4m3"):
    dtype, down = {"e4m3": (ml_dtypes.float8_e4m3fn, 7), "e5m2": (ml_dtypes.float8_e5m2, 14)}[fmt]
    v = np.moveaxis(np.asarray(x, np.float32).astype(ml_dtypes.bfloat16).astype(np.float64), axis, -1)
    blocks = v.reshape(v.shape[:-1] + (-1, 32))
    amax = np.abs(blocks).max(-1, keepdims=True)
    byte = np.maximum(np.where(amax > 0, np.frexp(amax)[1] - 1 + 127, 0) - down, 1)
    scale = np.exp2(byte - 127.0)
    codes = (blocks / scale).astype(np.float32).astype(dtype).astype(np.float64)
    return np.moveaxis((codes * scale).reshape(v.shape), -1, axis)


WIDE = False


def mx_kscale(k):
    if not WIDE:
        return np.ones(k)
    levels = np.array([10, -10, 5, -5, 0])
    if k % 512:
        return np.exp2(np.random.permutation(np.resize(levels, k // 32))).repeat(32)
    a = np.empty((k // 512, 16))
    for p in range(k // 512):
        a[p, :8] = np.random.permutation(np.resize(levels, 8))
        for g in range(8):
            far = levels[np.abs(levels - a[p, g]) >= 10]
            a[p, g + 8] = far[np.random.randint(len(far))]
    return np.exp2(a.ravel()).repeat(32)


def f64(x):
    return np.asarray(x).astype(np.float64)


def striped8(idx):
    return np.asarray(idx).reshape(8, -1, 16).transpose(0, 2, 1).reshape(128, -1).astype(np.uint16)


def unstriped8(offs):
    return offs.reshape(8, 16, -1).transpose(0, 2, 1).reshape(8, -1).astype(np.int64)


def pick8(x, idx, run):
    r = np.arange(len(x))
    return x[r[:, None], idx[r % (8 * run) // run]]


E2M1 = np.array([0.0, 0.5, 1.0, 1.5, 2.0, 3.0, 4.0, 6.0, -0.0, -0.5, -1.0, -1.5, -2.0, -3.0, -4.0, -6.0])


def pack_weight(w, fmt):
    k, n = w.shape
    w = f64(np.asarray(w, np.float32).astype(ml_dtypes.bfloat16)).reshape(k // 32, 32, n)
    amax = np.abs(w).max(1)
    if fmt == "e4m3":
        byte = np.frexp(amax)[1] - 1 + 127 - 7
    else:
        mant, ex = np.frexp(amax / 6.0)
        byte = np.where(mant > 0.5, ex, ex - 1) + 127
    byte = np.clip(np.where(amax > 0, byte, 1), 1, 254)
    scaled = (w * np.exp2(127.0 - byte)[:, None, :]).reshape(k, n).astype(np.float32)
    by_word = np.ascontiguousarray(scaled.reshape(k // 512, 128, 4, n).transpose(0, 1, 3, 2))
    if fmt == "e4m3":
        words = by_word.astype(ml_dtypes.float8_e4m3fn).view(np.uint8)
    else:
        c = by_word.astype(ml_dtypes.float4_e2m1fn).view(np.uint8) & 0xF
        words = (c[..., 0::2] | (c[..., 1::2] << 4)).reshape(k // 512, 128, 2 * n)
    return np.ascontiguousarray(words), np.ascontiguousarray(byte.astype(np.uint8).reshape(k // 512, 16, n))


def unpack_weight(words, scales, fmt):
    g, _, n = scales.shape
    words = np.ascontiguousarray(words).reshape(g, 128, n, -1)
    if fmt == "e4m3":
        vals = words.view(ml_dtypes.float8_e4m3fn).astype(np.float64)
    else:
        nib = np.empty((g, 128, n, 4), np.uint8)
        nib[..., 0::2] = words & 0xF
        nib[..., 1::2] = words >> 4
        vals = E2M1[nib]
    vals = vals * np.repeat(np.exp2(scales.astype(np.float64) - 127.0), 8, axis=1)[..., None]
    return vals.transpose(0, 1, 3, 2).reshape(g * 512, n)


D, K, T, U, I, J, Q = 512, 512, 1024, 1024, 512, 256, 128


def setup_inputs():
    n = np.random.standard_normal
    idx = np.stack([np.random.permutation(T)[:I] for _ in range(8)])
    idx2 = np.stack([np.random.permutation(U)[:I] for _ in range(8)])
    idx3 = np.stack([np.random.permutation(I)[:J] for _ in range(8)])
    idx4 = np.stack([np.random.permutation(I)[:J] for _ in range(8)])
    idx5 = np.stack([np.random.permutation(T)[:J] for _ in range(8)])
    idx6 = np.stack([np.random.permutation(T)[:I] for _ in range(8)])
    fd = mx_kscale(D)
    fk = mx_kscale(K)
    wqp = pack_weight(n((D, K)) * 1.0 / np.sqrt(D) * fd[:, None] * fk, "e4m3")
    cachep = pack_weight(n((K, T)) * 1.0 / np.sqrt(K) / fk[:, None], "e2m1")
    draftp = pack_weight(n((D, U)) * 1.0 / np.sqrt(D) * fd[:, None], "e4m3")
    return {
        "states": (n((D, Q)) * 0.95 / fd[:, None]).astype(np.float32),
        "wq_words": wqp[0],
        "wq_scales": wqp[1],
        "cache_words": cachep[0],
        "cache_scales": cachep[1],
        "draft_words": draftp[0],
        "draft_scales": draftp[1],
        "offs": striped8(idx),
        "offs2": striped8(idx2),
        "offs3": striped8(idx3),
        "offs4": striped8(idx4),
        "offs5": striped8(idx5),
        "offs6": striped8(idx6),
    }


def reference(states, wq_words, wq_scales, cache_words, cache_scales, draft_words, draft_scales, offs, offs2, offs3, offs4, offs5, offs6):
    idx = unstriped8(offs)
    idx2 = unstriped8(offs2)
    idx3 = unstriped8(offs3)
    idx4 = unstriped8(offs4)
    idx5 = unstriped8(offs5)
    idx6 = unstriped8(offs6)
    wqu = unpack_weight(wq_words, wq_scales, "e4m3")
    cacheu = unpack_weight(cache_words, cache_scales, "e2m1")
    draftu = unpack_weight(draft_words, draft_scales, "e4m3")
    statesq = mxq(f64(states), 0, "e4m3")
    qv = wqu.T @ statesq
    qvq = mxq(qv, 0, "e4m3")
    a = qvq.T @ cacheu
    b = statesq.T @ draftu
    w = pick8(a, idx, 16) - pick8(b, idx2, 16)
    p1 = np.maximum(pick8(w, idx3, 16), pick8(w, idx4, 16))
    f1 = np.zeros((Q, T))
    f1[np.arange(Q)[:, None], idx5[np.arange(Q) % 128 // 16]] = p1
    aa = a - f1
    y = pick8(aa, idx6, 16) + w
    return y

@@ -1,0 +1,181 @@
+from contextlib import ExitStack
+
+import concourse.mybir as mybir
+
+D, K, T, U, SLOTS, PICKS, Q = 512, 512, 1024, 1024, 512, 256, 128
+FLOPS = 2 * (D * K * Q + K * T * Q + D * U * Q)
+
+F32 = mybir.dt.float32
+BF16 = mybir.dt.bfloat16
+I32 = mybir.dt.int32
+U32 = mybir.dt.uint32
+U16 = mybir.dt.uint16
+U8 = mybir.dt.uint8
+FP8X4 = mybir.dt.float8_e4m3fn_x4
+FP4X4 = mybir.dt.float4_e2m1fn_x4
+COPY = mybir.ActivationFunctionType.Copy
+ALU = mybir.AluOpType
+
+P = 128
+PACK = 4
+BANK = 512
+PIECE = 256
+
+
+def load_scale_rows(nc, plane, scales):
+    for quad in range(4):
+        nc.sync.dma_start(
+            plane[32 * quad : 32 * quad + 4, :].bitcast(I32),
+            scales[0, 4 * quad : 4 * quad + 4, :].bitcast(I32),
+        )
+
+
+def tile_attend_bestslots_side_kernel(
+    tc, states, wq_words, wq_scales, cache_words, cache_scales, draft_words, draft_scales,
+    offs, offs2, offs3, offs4, offs5, offs6, out,
+):
+    nc = tc.nc
+    with ExitStack() as ctx:
+        lists = ctx.enter_context(tc.tile_pool(name="lists", bufs=1))
+        sb = ctx.enter_context(tc.tile_pool(name="sb", bufs=1))
+        psum = ctx.enter_context(tc.psum_pool(name="psum", bufs=1))
+
+        wq_plane_raw = sb.tile([P, K], U8, align_bytes=64)
+        draft_plane = sb.tile([P, U], U8, align_bytes=64)
+        cache_plane = sb.tile([P, T], U8, align_bytes=64)
+        f1 = sb.tile([P, T], F32, align_bytes=64)
+        nc.vector.memset(wq_plane_raw[:].bitcast(I32), 0)
+        nc.vector.memset(draft_plane[:].bitcast(I32), 0)
+        nc.vector.memset(cache_plane[:].bitcast(I32), 0)
+        nc.vector.memset(f1[:], 0.0)
+
+        states_raw = sb.tile([P, PACK, Q], F32, align_bytes=256)
+        wq_raw = sb.tile([P, K], U32, align_bytes=256)
+        draft_codes = sb.tile([P, U], U32, align_bytes=256)
+        cache_codes = sb.tile([P, 2 * T], U8, align_bytes=256)
+        nc.sync.dma_start(states_raw[:], states.rearrange("(p t) q -> p t q", t=PACK))
+        load_scale_rows(nc, wq_plane_raw, wq_scales)
+        nc.sync.dma_start(wq_raw[:].bitcast(I32), wq_words[0].rearrange("p n t -> p (n t)").bitcast(I32))
+        nc.sync.dma_start(draft_codes[:].bitcast(I32), draft_words[0].rearrange("p n t -> p (n t)").bitcast(I32))
+        load_scale_rows(nc, draft_plane, draft_scales)
+        nc.sync.dma_start(cache_codes[:].bitcast(I32), cache_words[0].bitcast(I32))
+        load_scale_rows(nc, cache_plane, cache_scales)
+        idx2 = lists.tile([P, SLOTS // 16], U16)
+        idx = lists.tile([P, SLOTS // 16], U16)
+        idx3 = lists.tile([P, PICKS // 16], U16)
+        idx4 = lists.tile([P, PICKS // 16], U16)
+        idx5 = lists.tile([P, PICKS // 16], U16)
+        idx6 = lists.tile([P, SLOTS // 16], U16)
+        for tile, source in ((idx2, offs2), (idx, offs), (idx3, offs3), (idx4, offs4), (idx5, offs5), (idx6, offs6)):
+            nc.sync.dma_start(tile[:], source)
+
+        states_bf = sb.tile([P, Q, PACK], BF16, align_bytes=64)
+        half_q = Q // 2
+        nc.vector.tensor_copy(
+            states_bf[:, :half_q, :].rearrange("p (c i) t -> p c t i", i=4),
+            states_raw[:, :, :half_q].rearrange("p t (c i) -> p c t i", i=4),
+        )
+        nc.scalar.activation(
+            states_bf[:, half_q:, :].rearrange("p (c i) t -> p c t i", i=4),
+            states_raw[:, :, half_q:].rearrange("p t (c i) -> p c t i", i=4),
+            COPY,
+        )
+        wq_plane = sb.tile([P, PACK, P], U8, align_bytes=64)
+        nc.vector.tensor_copy(
+            wq_plane[:].rearrange("p t (c i) -> p c t i", i=16),
+            wq_plane_raw[:].rearrange("p (c i t) -> p c t i", i=16, t=PACK),
+        )
+        states_codes = sb.tile([P, Q], U32, align_bytes=64)
+        states_plane = sb.tile([P, Q], U8, align_bytes=64)
+        nc.vector.quantize_mx(states_codes[:].bitcast(FP8X4), states_plane[:], states_bf[:].rearrange("p q t -> p (q t)"))
+
+        wq_low = sb.tile([P, 2, P], U32, align_bytes=64)
+        wq_high = sb.tile([P, 2, P], U32, align_bytes=64)
+        nc.vector.tensor_copy(
+            wq_low[:].bitcast(I32).rearrange("p t (c i) -> p c t i", i=4),
+            wq_raw[:].bitcast(I32).rearrange("p (c i t) -> p c t i", i=4, t=PACK)[:, :, 0:2, :],
+        )
+        nc.scalar.copy(
+            wq_high[:].rearrange("p t (c i) -> p c t i", i=4),
+            wq_raw[:].rearrange("p (c i t) -> p c t i", i=4, t=PACK)[:, :, 2:4, :],
+        )
+
+        qv_bank = psum.tile([P, PACK, Q], F32)
+        for t in range(PACK):
+            dealt = wq_low if t < 2 else wq_high
+            nc.tensor.matmul_mx(
+                qv_bank[:, t, :],
+                lhsT=dealt[:, t % 2, :].bitcast(FP8X4), lhsT_scale=wq_plane[:, t, :],
+                rhs=states_codes[:].bitcast(FP8X4), rhs_scale=states_plane[:],
+                start=True, stop=True,
+            )
+        b_banks = [psum.tile([P, BANK], F32, name=f"b_bank{n}") for n in range(U // BANK)]
+        for n, bank in enumerate(b_banks):
+            cols = slice(n * BANK, (n + 1) * BANK)
+            nc.tensor.matmul_mx(
+                bank[:],
+                lhsT=states_codes[:].bitcast(FP8X4), lhsT_scale=states_plane[:],
+                rhs=draft_codes[:, cols].bitcast(FP8X4), rhs_scale=draft_plane[:, cols],
+                start=True, stop=True,
+            )
+
+        qv_bf = sb.tile([P, Q, PACK], BF16, align_bytes=64)
+        nc.vector.tensor_copy(qv_bf[:], qv_bank[:].rearrange("p t q -> p q t"))
+        qv_codes = sb.tile([P, Q], U32, align_bytes=64)
+        qv_plane = sb.tile([P, Q], U8, align_bytes=64)
+        nc.vector.quantize_mx(qv_codes[:].bitcast(FP8X4), qv_plane[:], qv_bf[:].rearrange("p q t -> p (q t)"))
+
+        b = sb.tile([P, U], F32, align_bytes=64)
+        nc.scalar.copy(b[:, :BANK], b_banks[0][:])
+        nc.vector.tensor_copy(b[:, BANK:], b_banks[1][:])
+
+        a_banks = [psum.tile([P, PIECE], F32, name=f"a_bank{n}") for n in range(T // PIECE)]
+        for n, bank in enumerate(a_banks):
+            nc.tensor.matmul_mx(
+                bank[:],
+                lhsT=qv_codes[:].bitcast(FP8X4), lhsT_scale=qv_plane[:],
+                rhs=cache_codes[:, 2 * n * PIECE : 2 * (n + 1) * PIECE].bitcast(FP4X4),
+                rhs_scale=cache_plane[:, n * PIECE : (n + 1) * PIECE],
+                start=True, stop=True,
+            )
+
+        half = SLOTS // 2
+        hc = half // 16
+        b_first = sb.tile([P, half], F32, align_bytes=64)
+        b_second = sb.tile([P, half], F32, align_bytes=64)
+        nc.scalar.activation(b_first[:], b[:].indirect(idx2[:, :hc]), COPY)
+
+        a = sb.tile([P, T], F32, align_bytes=64)
+        for n, bank in enumerate(a_banks):
+            cols = slice(n * PIECE, (n + 1) * PIECE)
+            if n % 2 == 0:
+                nc.vector.tensor_copy(a[:, cols], bank[:])
+            else:
+                nc.scalar.copy(a[:, cols], bank[:])
+        nc.vector.tensor_copy(b_second[:], b[:].indirect(idx2[:, hc:]))
+
+        w = sb.tile([P, SLOTS], F32, align_bytes=64)
+        a_second = sb.tile([P, half], F32, align_bytes=64)
+        nc.vector.tensor_tensor(w[:, :half], a[:].indirect(idx[:, :hc]), b_first[:], ALU.subtract)
+        nc.scalar.activation(a_second[:], a[:].indirect(idx[:, hc:]), COPY)
+        nc.vector.tensor_tensor(w[:, half:], a_second[:], b_second[:], ALU.subtract)
+
+        lead3 = sb.tile([P, PICKS], F32, align_bytes=64)
+        lead4 = sb.tile([P, PICKS], F32, align_bytes=64)
+        p1 = sb.tile([P, PICKS], F32, align_bytes=64)
+        nc.vector.tensor_copy(lead3[:], w[:].indirect(idx3[:]))
+        nc.scalar.activation(lead4[:], w[:].indirect(idx4[:]), COPY)
+        nc.vector.tensor_tensor(p1[:], lead3[:], lead4[:], ALU.max)
+        nc.scalar.activation(f1[:].indirect(idx5[:]), p1[:], COPY)
+
+        aa = sb.tile([P, T], F32, align_bytes=64)
+        nc.vector.tensor_tensor(aa[:], a[:], f1[:], ALU.subtract)
+
+        y_first = sb.tile([P, half], F32, align_bytes=64)
+        y_second = sb.tile([P, half], F32, align_bytes=64)
+        aa_second = sb.tile([P, half], F32, align_bytes=64)
+        nc.vector.tensor_tensor(y_first[:], aa[:].indirect(idx6[:, :hc]), w[:, :half], ALU.add)
+        nc.scalar.activation(aa_second[:], aa[:].indirect(idx6[:, hc:]), COPY)
+        nc.sync.dma_start(out[:, :half], y_first[:])
+        nc.vector.tensor_tensor(y_second[:], aa_second[:], w[:, half:], ALU.add)
+        nc.sync.dma_start(out[:, half:], y_second[:])

@@ -22,8 +22,8 @@ BANK = 512
 PIECE = 256
 
 
-def load_scale_rows(nc, plane, scales):
-    for quad in range(4):
+def load_scale_rows(nc, plane, scales, quads=range(4)):
+    for quad in quads:
         nc.sync.dma_start(
             plane[32 * quad : 32 * quad + 4, :].bitcast(I32),
             scales[0, 4 * quad : 4 * quad + 4, :].bitcast(I32),
@@ -41,11 +41,12 @@ def tile_attend_bestslots_side_kernel(
         psum = ctx.enter_context(tc.psum_pool(name="psum", bufs=1))
 
         wq_plane_raw = sb.tile([P, K], U8, align_bytes=64)
-        draft_plane = sb.tile([P, U], U8, align_bytes=64)
+        draft_rows = sb.tile([P, 2 * U], U8, align_bytes=64)
+        draft_plane = draft_rows[:, :U]
         cache_plane = sb.tile([P, T], U8, align_bytes=64)
         f1 = sb.tile([P, T], F32, align_bytes=64)
         nc.vector.memset(wq_plane_raw[:].bitcast(I32), 0)
-        nc.vector.memset(draft_plane[:].bitcast(I32), 0)
+        nc.gpsimd.memset(draft_plane.bitcast(I32), 0)
         nc.vector.memset(cache_plane[:].bitcast(I32), 0)
         nc.vector.memset(f1[:], 0.0)
 
@@ -54,10 +55,14 @@ def tile_attend_bestslots_side_kernel(
         draft_codes = sb.tile([P, U], U32, align_bytes=256)
         cache_codes = sb.tile([P, 2 * T], U8, align_bytes=256)
         nc.sync.dma_start(states_raw[:], states.rearrange("(p t) q -> p t q", t=PACK))
-        load_scale_rows(nc, wq_plane_raw, wq_scales)
         nc.sync.dma_start(wq_raw[:].bitcast(I32), wq_words[0].rearrange("p n t -> p (n t)").bitcast(I32))
+        load_scale_rows(nc, wq_plane_raw, wq_scales)
+        nc.sync.dma_start(
+            draft_rows[0:4, :].bitcast(I32).rearrange("r (h c) -> r h c", h=2),
+            draft_scales[0, 0:8, :].bitcast(I32).rearrange("(h r) c -> r h c", h=2),
+        )
         nc.sync.dma_start(draft_codes[:].bitcast(I32), draft_words[0].rearrange("p n t -> p (n t)").bitcast(I32))
-        load_scale_rows(nc, draft_plane, draft_scales)
+        load_scale_rows(nc, draft_plane, draft_scales, range(2, 4))
         nc.sync.dma_start(cache_codes[:].bitcast(I32), cache_words[0].bitcast(I32))
         load_scale_rows(nc, cache_plane, cache_scales)
         idx2 = lists.tile([P, SLOTS // 16], U16)
@@ -80,27 +85,23 @@ def tile_attend_bestslots_side_kernel(
             states_raw[:, :, half_q:].rearrange("p t (c i) -> p c t i", i=4),
             COPY,
         )
-        wq_plane = sb.tile([P, PACK, P], U8, align_bytes=64)
-        nc.vector.tensor_copy(
-            wq_plane[:].rearrange("p t (c i) -> p c t i", i=16),
-            wq_plane_raw[:].rearrange("p (c i t) -> p c t i", i=16, t=PACK),
-        )
         states_codes = sb.tile([P, Q], U32, align_bytes=64)
         states_plane = sb.tile([P, Q], U8, align_bytes=64)
         nc.vector.quantize_mx(states_codes[:].bitcast(FP8X4), states_plane[:], states_bf[:].rearrange("p q t -> p (q t)"))
 
+        wq_plane = sb.tile([P, PACK, P], U8, align_bytes=64)
+        for t in range(PACK):
+            nc.vector.tensor_copy(wq_plane[:, t, :], wq_plane_raw[:, t:K:PACK])
         wq_low = sb.tile([P, 2, P], U32, align_bytes=64)
         wq_high = sb.tile([P, 2, P], U32, align_bytes=64)
-        nc.vector.tensor_copy(
-            wq_low[:].bitcast(I32).rearrange("p t (c i) -> p c t i", i=4),
-            wq_raw[:].bitcast(I32).rearrange("p (c i t) -> p c t i", i=4, t=PACK)[:, :, 0:2, :],
-        )
-        nc.scalar.copy(
-            wq_high[:].rearrange("p t (c i) -> p c t i", i=4),
-            wq_raw[:].rearrange("p (c i t) -> p c t i", i=4, t=PACK)[:, :, 2:4, :],
-        )
+        for pair, dealt in enumerate((wq_low, wq_high)):
+            nc.scalar.copy(
+                dealt[:].rearrange("p t (c i) -> p c t i", i=4),
+                wq_raw[:].rearrange("p (c i t) -> p c t i", i=4, t=PACK)[:, :, 2 * pair : 2 * pair + 2, :],
+            )
+        nc.vector.tensor_copy(draft_rows[32:36, :U].bitcast(I32), draft_rows[0:4, U:].bitcast(I32))
 
-        qv_bank = psum.tile([P, PACK, Q], F32)
+        qv_bank = psum.tile([P, PACK, Q], F32, tag="shared")
         for t in range(PACK):
             dealt = wq_low if t < 2 else wq_high
             nc.tensor.matmul_mx(
@@ -109,13 +110,13 @@ def tile_attend_bestslots_side_kernel(
                 rhs=states_codes[:].bitcast(FP8X4), rhs_scale=states_plane[:],
                 start=True, stop=True,
             )
-        b_banks = [psum.tile([P, BANK], F32, name=f"b_bank{n}") for n in range(U // BANK)]
+        b_banks = [psum.tile([P, PIECE], F32, name=f"b_bank{n}") for n in range(U // PIECE)]
         for n, bank in enumerate(b_banks):
-            cols = slice(n * BANK, (n + 1) * BANK)
+            cols = slice(n * PIECE, (n + 1) * PIECE)
             nc.tensor.matmul_mx(
                 bank[:],
                 lhsT=states_codes[:].bitcast(FP8X4), lhsT_scale=states_plane[:],
-                rhs=draft_codes[:, cols].bitcast(FP8X4), rhs_scale=draft_plane[:, cols],
+                rhs=draft_codes[:, cols].bitcast(FP8X4), rhs_scale=draft_rows[:, cols],
                 start=True, stop=True,
             )
 
@@ -126,10 +127,11 @@ def tile_attend_bestslots_side_kernel(
         nc.vector.quantize_mx(qv_codes[:].bitcast(FP8X4), qv_plane[:], qv_bf[:].rearrange("p q t -> p (q t)"))
 
         b = sb.tile([P, U], F32, align_bytes=64)
-        nc.scalar.copy(b[:, :BANK], b_banks[0][:])
-        nc.vector.tensor_copy(b[:, BANK:], b_banks[1][:])
+        for n, bank in enumerate(b_banks):
+            nc.scalar.copy(b[:, n * PIECE : (n + 1) * PIECE], bank[:])
 
-        a_banks = [psum.tile([P, PIECE], F32, name=f"a_bank{n}") for n in range(T // PIECE)]
+        a_banks = [psum.tile([P, PIECE], F32, name=f"a_bank{n}") for n in range(T // PIECE - 1)]
+        a_banks.append(psum.tile([P, PIECE], F32, name="a_bank_last", tag="shared"))
         for n, bank in enumerate(a_banks):
             nc.tensor.matmul_mx(
                 bank[:],
@@ -148,11 +150,8 @@ def tile_attend_bestslots_side_kernel(
         a = sb.tile([P, T], F32, align_bytes=64)
         for n, bank in enumerate(a_banks):
             cols = slice(n * PIECE, (n + 1) * PIECE)
-            if n % 2 == 0:
-                nc.vector.tensor_copy(a[:, cols], bank[:])
-            else:
-                nc.scalar.copy(a[:, cols], bank[:])
-        nc.vector.tensor_copy(b_second[:], b[:].indirect(idx2[:, hc:]))
+            nc.vector.tensor_copy(a[:, cols], bank[:])
+        nc.scalar.activation(b_second[:], b[:].indirect(idx2[:, hc:]), COPY)
 
         w = sb.tile([P, SLOTS], F32, align_bytes=64)
         a_second = sb.tile([P, half], F32, align_bytes=64)
@@ -169,7 +168,12 @@ def tile_attend_bestslots_side_kernel(
         nc.scalar.activation(f1[:].indirect(idx5[:]), p1[:], COPY)
 
         aa = sb.tile([P, T], F32, align_bytes=64)
-        nc.vector.tensor_tensor(aa[:], a[:], f1[:], ALU.subtract)
+        split = 688
+        for n, bank in enumerate(a_banks):
+            lo, hi = n * PIECE, min((n + 1) * PIECE, split)
+            if lo < hi:
+                nc.vector.tensor_tensor(aa[:, lo:hi], bank[:, : hi - lo], f1[:, lo:hi], ALU.subtract)
+        nc.gpsimd.tensor_tensor(aa[:, split:], a[:, split:], f1[:, split:], ALU.subtract)
 
         y_first = sb.tile([P, half], F32, align_bytes=64)
         y_second = sb.tile([P, half], F32, align_bytes=64)

@@ -41,12 +41,11 @@ def tile_attend_bestslots_side_kernel(
         psum = ctx.enter_context(tc.psum_pool(name="psum", bufs=1))
 
         wq_plane_raw = sb.tile([P, K], U8, align_bytes=64)
-        draft_rows = sb.tile([P, 2 * U], U8, align_bytes=64)
-        draft_plane = draft_rows[:, :U]
+        draft_plane = sb.tile([P, U], U8, align_bytes=64)
         cache_plane = sb.tile([P, T], U8, align_bytes=64)
         f1 = sb.tile([P, T], F32, align_bytes=64)
         nc.vector.memset(wq_plane_raw[:].bitcast(I32), 0)
-        nc.gpsimd.memset(draft_plane.bitcast(I32), 0)
+        nc.gpsimd.memset(draft_plane[:].bitcast(I32), 0)
         nc.vector.memset(cache_plane[:].bitcast(I32), 0)
         nc.vector.memset(f1[:], 0.0)
 
@@ -57,12 +56,10 @@ def tile_attend_bestslots_side_kernel(
         nc.sync.dma_start(states_raw[:], states.rearrange("(p t) q -> p t q", t=PACK))
         nc.sync.dma_start(wq_raw[:].bitcast(I32), wq_words[0].rearrange("p n t -> p (n t)").bitcast(I32))
         load_scale_rows(nc, wq_plane_raw, wq_scales)
-        nc.sync.dma_start(
-            draft_rows[0:4, :].bitcast(I32).rearrange("r (h c) -> r h c", h=2),
-            draft_scales[0, 0:8, :].bitcast(I32).rearrange("(h r) c -> r h c", h=2),
-        )
+        draft_staged = sb.tile([4, 3, U // 4], I32, align_bytes=64, tag="staged_then_qv")
+        nc.sync.dma_start(draft_staged[:], draft_scales[0, 0:12, :].bitcast(I32).rearrange("(h r) c -> r h c", h=3))
         nc.sync.dma_start(draft_codes[:].bitcast(I32), draft_words[0].rearrange("p n t -> p (n t)").bitcast(I32))
-        load_scale_rows(nc, draft_plane, draft_scales, range(2, 4))
+        load_scale_rows(nc, draft_plane, draft_scales, range(3, 4))
         nc.sync.dma_start(cache_codes[:].bitcast(I32), cache_words[0].bitcast(I32))
         load_scale_rows(nc, cache_plane, cache_scales)
         idx2 = lists.tile([P, SLOTS // 16], U16)
@@ -99,7 +96,9 @@ def tile_attend_bestslots_side_kernel(
                 dealt[:].rearrange("p t (c i) -> p c t i", i=4),
                 wq_raw[:].rearrange("p (c i t) -> p c t i", i=4, t=PACK)[:, :, 2 * pair : 2 * pair + 2, :],
             )
-        nc.vector.tensor_copy(draft_rows[32:36, :U].bitcast(I32), draft_rows[0:4, U:].bitcast(I32))
+        nc.scalar.copy(draft_plane[0:4, :].bitcast(U32), draft_staged[:, 0, :].bitcast(U32))
+        for quad in (1, 2):
+            nc.vector.tensor_copy(draft_plane[32 * quad : 32 * quad + 4, :].bitcast(I32), draft_staged[:, quad, :])
 
         qv_bank = psum.tile([P, PACK, Q], F32, tag="shared")
         for t in range(PACK):
@@ -116,11 +115,11 @@ def tile_attend_bestslots_side_kernel(
             nc.tensor.matmul_mx(
                 bank[:],
                 lhsT=states_codes[:].bitcast(FP8X4), lhsT_scale=states_plane[:],
-                rhs=draft_codes[:, cols].bitcast(FP8X4), rhs_scale=draft_rows[:, cols],
+                rhs=draft_codes[:, cols].bitcast(FP8X4), rhs_scale=draft_plane[:, cols],
                 start=True, stop=True,
             )
 
-        qv_bf = sb.tile([P, Q, PACK], BF16, align_bytes=64)
+        qv_bf = sb.tile([P, Q, PACK], BF16, align_bytes=64, tag="staged_then_qv")
         nc.vector.tensor_copy(qv_bf[:], qv_bank[:].rearrange("p t q -> p q t"))
         qv_codes = sb.tile([P, Q], U32, align_bytes=64)
         qv_plane = sb.tile([P, Q], U8, align_bytes=64)
@@ -162,10 +161,12 @@ def tile_attend_bestslots_side_kernel(
         lead3 = sb.tile([P, PICKS], F32, align_bytes=64)
         lead4 = sb.tile([P, PICKS], F32, align_bytes=64)
         p1 = sb.tile([P, PICKS], F32, align_bytes=64)
-        nc.vector.tensor_copy(lead3[:], w[:].indirect(idx3[:]))
-        nc.scalar.activation(lead4[:], w[:].indirect(idx4[:]), COPY)
-        nc.vector.tensor_tensor(p1[:], lead3[:], lead4[:], ALU.max)
-        nc.scalar.activation(f1[:].indirect(idx5[:]), p1[:], COPY)
+        for lo, hi in ((0, PICKS // 2), (PICKS // 2, PICKS)):
+            nc.vector.tensor_copy(lead3[:, lo:hi], w[:].indirect(idx3[:, lo // 16 : hi // 16]))
+            nc.scalar.activation(lead4[:, lo:hi], w[:].indirect(idx4[:, lo // 16 : hi // 16]), COPY)
+        for lo, hi in ((0, 64), (64, PICKS)):
+            nc.vector.tensor_tensor(p1[:, lo:hi], lead3[:, lo:hi], lead4[:, lo:hi], ALU.max)
+            nc.scalar.activation(f1[:].indirect(idx5[:, lo // 16 : hi // 16]), p1[:, lo:hi], COPY)
 
         aa = sb.tile([P, T], F32, align_bytes=64)
         split = 688

@@ -41,11 +41,12 @@ def tile_attend_bestslots_side_kernel(
         psum = ctx.enter_context(tc.psum_pool(name="psum", bufs=1))
 
         wq_plane_raw = sb.tile([P, K], U8, align_bytes=64)
-        draft_plane = sb.tile([P, U], U8, align_bytes=64)
+        draft_rows = sb.tile([P, 2 * U], U8, align_bytes=64)
+        draft_plane = draft_rows[:, :U]
         cache_plane = sb.tile([P, T], U8, align_bytes=64)
         f1 = sb.tile([P, T], F32, align_bytes=64)
         nc.vector.memset(wq_plane_raw[:].bitcast(I32), 0)
-        nc.gpsimd.memset(draft_plane[:].bitcast(I32), 0)
+        nc.gpsimd.memset(draft_plane.bitcast(I32), 0)
         nc.vector.memset(cache_plane[:].bitcast(I32), 0)
         nc.vector.memset(f1[:], 0.0)
 
@@ -56,10 +57,12 @@ def tile_attend_bestslots_side_kernel(
         nc.sync.dma_start(states_raw[:], states.rearrange("(p t) q -> p t q", t=PACK))
         nc.sync.dma_start(wq_raw[:].bitcast(I32), wq_words[0].rearrange("p n t -> p (n t)").bitcast(I32))
         load_scale_rows(nc, wq_plane_raw, wq_scales)
-        draft_staged = sb.tile([4, 3, U // 4], I32, align_bytes=64, tag="staged_then_qv")
-        nc.sync.dma_start(draft_staged[:], draft_scales[0, 0:12, :].bitcast(I32).rearrange("(h r) c -> r h c", h=3))
+        nc.sync.dma_start(
+            draft_rows[0:4, :].bitcast(I32).rearrange("r (h c) -> r h c", h=2),
+            draft_scales[0, 0:8, :].bitcast(I32).rearrange("(h r) c -> r h c", h=2),
+        )
         nc.sync.dma_start(draft_codes[:].bitcast(I32), draft_words[0].rearrange("p n t -> p (n t)").bitcast(I32))
-        load_scale_rows(nc, draft_plane, draft_scales, range(3, 4))
+        load_scale_rows(nc, draft_plane, draft_scales, range(2, 4))
         nc.sync.dma_start(cache_codes[:].bitcast(I32), cache_words[0].bitcast(I32))
         load_scale_rows(nc, cache_plane, cache_scales)
         idx2 = lists.tile([P, SLOTS // 16], U16)
@@ -96,9 +99,7 @@ def tile_attend_bestslots_side_kernel(
                 dealt[:].rearrange("p t (c i) -> p c t i", i=4),
                 wq_raw[:].rearrange("p (c i t) -> p c t i", i=4, t=PACK)[:, :, 2 * pair : 2 * pair + 2, :],
             )
-        nc.scalar.copy(draft_plane[0:4, :].bitcast(U32), draft_staged[:, 0, :].bitcast(U32))
-        for quad in (1, 2):
-            nc.vector.tensor_copy(draft_plane[32 * quad : 32 * quad + 4, :].bitcast(I32), draft_staged[:, quad, :])
+        nc.vector.tensor_copy(draft_rows[32:36, :U].bitcast(I32), draft_rows[0:4, U:].bitcast(I32))
 
         qv_bank = psum.tile([P, PACK, Q], F32, tag="shared")
         for t in range(PACK):
@@ -115,11 +116,11 @@ def tile_attend_bestslots_side_kernel(
             nc.tensor.matmul_mx(
                 bank[:],
                 lhsT=states_codes[:].bitcast(FP8X4), lhsT_scale=states_plane[:],
-                rhs=draft_codes[:, cols].bitcast(FP8X4), rhs_scale=draft_plane[:, cols],
+                rhs=draft_codes[:, cols].bitcast(FP8X4), rhs_scale=draft_rows[:, cols],
                 start=True, stop=True,
             )
 
-        qv_bf = sb.tile([P, Q, PACK], BF16, align_bytes=64, tag="staged_then_qv")
+        qv_bf = sb.tile([P, Q, PACK], BF16, align_bytes=64)
         nc.vector.tensor_copy(qv_bf[:], qv_bank[:].rearrange("p t q -> p q t"))
         qv_codes = sb.tile([P, Q], U32, align_bytes=64)
         qv_plane = sb.tile([P, Q], U8, align_bytes=64)

from contextlib import ExitStack

import concourse.mybir as mybir

D, K, T, U, SLOTS, PICKS, Q = 512, 512, 1024, 1024, 512, 256, 128
FLOPS = 2 * (D * K * Q + K * T * Q + D * U * Q)

F32 = mybir.dt.float32
BF16 = mybir.dt.bfloat16
I32 = mybir.dt.int32
U32 = mybir.dt.uint32
U16 = mybir.dt.uint16
U8 = mybir.dt.uint8
FP8X4 = mybir.dt.float8_e4m3fn_x4
FP4X4 = mybir.dt.float4_e2m1fn_x4
COPY = mybir.ActivationFunctionType.Copy
ALU = mybir.AluOpType

P = 128
PACK = 4
BANK = 512
PIECE = 256


def load_scale_rows(nc, plane, scales, quads=range(4)):
    for quad in quads:
        nc.sync.dma_start(
            plane[32 * quad : 32 * quad + 4, :].bitcast(I32),
            scales[0, 4 * quad : 4 * quad + 4, :].bitcast(I32),
        )


def tile_attend_bestslots_side_kernel(
    tc, states, wq_words, wq_scales, cache_words, cache_scales, draft_words, draft_scales,
    offs, offs2, offs3, offs4, offs5, offs6, out,
):
    nc = tc.nc
    with ExitStack() as ctx:
        lists = ctx.enter_context(tc.tile_pool(name="lists", bufs=1))
        sb = ctx.enter_context(tc.tile_pool(name="sb", bufs=1))
        psum = ctx.enter_context(tc.psum_pool(name="psum", bufs=1))

        wq_plane_raw = sb.tile([P, K], U8, align_bytes=64)
        draft_rows = sb.tile([P, 2 * U], U8, align_bytes=64)
        draft_plane = draft_rows[:, :U]
        cache_plane = sb.tile([P, T], U8, align_bytes=64)
        f1 = sb.tile([P, T], F32, align_bytes=64)
        nc.vector.memset(wq_plane_raw[:].bitcast(I32), 0)
        nc.gpsimd.memset(draft_plane.bitcast(I32), 0)
        nc.vector.memset(cache_plane[:].bitcast(I32), 0)
        nc.vector.memset(f1[:], 0.0)

        states_raw = sb.tile([P, PACK, Q], F32, align_bytes=256)
        wq_raw = sb.tile([P, K], U32, align_bytes=256)
        draft_codes = sb.tile([P, U], U32, align_bytes=256)
        cache_codes = sb.tile([P, 2 * T], U8, align_bytes=256)
        nc.sync.dma_start(states_raw[:], states.rearrange("(p t) q -> p t q", t=PACK))
        nc.sync.dma_start(wq_raw[:].bitcast(I32), wq_words[0].rearrange("p n t -> p (n t)").bitcast(I32))
        load_scale_rows(nc, wq_plane_raw, wq_scales)
        nc.sync.dma_start(
            draft_rows[0:4, :].bitcast(I32).rearrange("r (h c) -> r h c", h=2),
            draft_scales[0, 0:8, :].bitcast(I32).rearrange("(h r) c -> r h c", h=2),
        )
        nc.sync.dma_start(draft_codes[:].bitcast(I32), draft_words[0].rearrange("p n t -> p (n t)").bitcast(I32))
        load_scale_rows(nc, draft_plane, draft_scales, range(2, 4))
        nc.sync.dma_start(cache_codes[:].bitcast(I32), cache_words[0].bitcast(I32))
        load_scale_rows(nc, cache_plane, cache_scales)
        idx2 = lists.tile([P, SLOTS // 16], U16)
        idx = lists.tile([P, SLOTS // 16], U16)
        idx3 = lists.tile([P, PICKS // 16], U16)
        idx4 = lists.tile([P, PICKS // 16], U16)
        idx5 = lists.tile([P, PICKS // 16], U16)
        idx6 = lists.tile([P, SLOTS // 16], U16)
        for tile, source in ((idx2, offs2), (idx, offs), (idx3, offs3), (idx4, offs4), (idx5, offs5), (idx6, offs6)):
            nc.sync.dma_start(tile[:], source)

        states_bf = sb.tile([P, Q, PACK], BF16, align_bytes=64)
        half_q = Q // 2
        nc.vector.tensor_copy(
            states_bf[:, :half_q, :].rearrange("p (c i) t -> p c t i", i=4),
            states_raw[:, :, :half_q].rearrange("p t (c i) -> p c t i", i=4),
        )
        nc.scalar.activation(
            states_bf[:, half_q:, :].rearrange("p (c i) t -> p c t i", i=4),
            states_raw[:, :, half_q:].rearrange("p t (c i) -> p c t i", i=4),
            COPY,
        )
        states_codes = sb.tile([P, Q], U32, align_bytes=64)
        states_plane = sb.tile([P, Q], U8, align_bytes=64)
        nc.vector.quantize_mx(states_codes[:].bitcast(FP8X4), states_plane[:], states_bf[:].rearrange("p q t -> p (q t)"))

        wq_plane = sb.tile([P, PACK, P], U8, align_bytes=64)
        for t in range(PACK):
            nc.vector.tensor_copy(wq_plane[:, t, :], wq_plane_raw[:, t:K:PACK])
        wq_low = sb.tile([P, 2, P], U32, align_bytes=64)
        wq_high = sb.tile([P, 2, P], U32, align_bytes=64)
        for pair, dealt in enumerate((wq_low, wq_high)):
            nc.scalar.copy(
                dealt[:].rearrange("p t (c i) -> p c t i", i=4),
                wq_raw[:].rearrange("p (c i t) -> p c t i", i=4, t=PACK)[:, :, 2 * pair : 2 * pair + 2, :],
            )
        nc.vector.tensor_copy(draft_rows[32:36, :U].bitcast(I32), draft_rows[0:4, U:].bitcast(I32))

        qv_bank = psum.tile([P, PACK, Q], F32, tag="shared")
        for t in range(PACK):
            dealt = wq_low if t < 2 else wq_high
            nc.tensor.matmul_mx(
                qv_bank[:, t, :],
                lhsT=dealt[:, t % 2, :].bitcast(FP8X4), lhsT_scale=wq_plane[:, t, :],
                rhs=states_codes[:].bitcast(FP8X4), rhs_scale=states_plane[:],
                start=True, stop=True,
            )
        b_banks = [psum.tile([P, PIECE], F32, name=f"b_bank{n}") for n in range(U // PIECE)]
        for n, bank in enumerate(b_banks):
            cols = slice(n * PIECE, (n + 1) * PIECE)
            nc.tensor.matmul_mx(
                bank[:],
                lhsT=states_codes[:].bitcast(FP8X4), lhsT_scale=states_plane[:],
                rhs=draft_codes[:, cols].bitcast(FP8X4), rhs_scale=draft_rows[:, cols],
                start=True, stop=True,
            )

        qv_bf = sb.tile([P, Q, PACK], BF16, align_bytes=64)
        nc.vector.tensor_copy(qv_bf[:], qv_bank[:].rearrange("p t q -> p q t"))
        qv_codes = sb.tile([P, Q], U32, align_bytes=64)
        qv_plane = sb.tile([P, Q], U8, align_bytes=64)
        nc.vector.quantize_mx(qv_codes[:].bitcast(FP8X4), qv_plane[:], qv_bf[:].rearrange("p q t -> p (q t)"))

        b = sb.tile([P, U], F32, align_bytes=64)
        for n, bank in enumerate(b_banks):
            nc.scalar.copy(b[:, n * PIECE : (n + 1) * PIECE], bank[:])

        a_banks = [psum.tile([P, PIECE], F32, name=f"a_bank{n}") for n in range(T // PIECE - 1)]
        a_banks.append(psum.tile([P, PIECE], F32, name="a_bank_last", tag="shared"))
        for n, bank in enumerate(a_banks):
            nc.tensor.matmul_mx(
                bank[:],
                lhsT=qv_codes[:].bitcast(FP8X4), lhsT_scale=qv_plane[:],
                rhs=cache_codes[:, 2 * n * PIECE : 2 * (n + 1) * PIECE].bitcast(FP4X4),
                rhs_scale=cache_plane[:, n * PIECE : (n + 1) * PIECE],
                start=True, stop=True,
            )

        half = SLOTS // 2
        hc = half // 16
        b_first = sb.tile([P, half], F32, align_bytes=64)
        b_second = sb.tile([P, half], F32, align_bytes=64)
        nc.scalar.activation(b_first[:], b[:].indirect(idx2[:, :hc]), COPY)

        a = sb.tile([P, T], F32, align_bytes=64)
        for n, bank in enumerate(a_banks):
            cols = slice(n * PIECE, (n + 1) * PIECE)
            nc.vector.tensor_copy(a[:, cols], bank[:])
        nc.scalar.activation(b_second[:], b[:].indirect(idx2[:, hc:]), COPY)

        w = sb.tile([P, SLOTS], F32, align_bytes=64)
        a_second = sb.tile([P, half], F32, align_bytes=64)
        nc.vector.tensor_tensor(w[:, :half], a[:].indirect(idx[:, :hc]), b_first[:], ALU.subtract)
        nc.scalar.activation(a_second[:], a[:].indirect(idx[:, hc:]), COPY)
        nc.vector.tensor_tensor(w[:, half:], a_second[:], b_second[:], ALU.subtract)

        lead3 = sb.tile([P, PICKS], F32, align_bytes=64)
        lead4 = sb.tile([P, PICKS], F32, align_bytes=64)
        p1 = sb.tile([P, PICKS], F32, align_bytes=64)
        for lo, hi in ((0, PICKS // 2), (PICKS // 2, PICKS)):
            nc.vector.tensor_copy(lead3[:, lo:hi], w[:].indirect(idx3[:, lo // 16 : hi // 16]))
            nc.scalar.activation(lead4[:, lo:hi], w[:].indirect(idx4[:, lo // 16 : hi // 16]), COPY)
        for lo, hi in ((0, 64), (64, PICKS)):
            nc.vector.tensor_tensor(p1[:, lo:hi], lead3[:, lo:hi], lead4[:, lo:hi], ALU.max)
            nc.scalar.activation(f1[:].indirect(idx5[:, lo // 16 : hi // 16]), p1[:, lo:hi], COPY)

        aa = sb.tile([P, T], F32, align_bytes=64)
        split = 688
        for n, bank in enumerate(a_banks):
            lo, hi = n * PIECE, min((n + 1) * PIECE, split)
            if lo < hi:
                nc.vector.tensor_tensor(aa[:, lo:hi], bank[:, : hi - lo], f1[:, lo:hi], ALU.subtract)
        nc.gpsimd.tensor_tensor(aa[:, split:], a[:, split:], f1[:, split:], ALU.subtract)

        y_first = sb.tile([P, half], F32, align_bytes=64)
        y_second = sb.tile([P, half], F32, align_bytes=64)
        aa_second = sb.tile([P, half], F32, align_bytes=64)
        nc.vector.tensor_tensor(y_first[:], aa[:].indirect(idx6[:, :hc]), w[:, :half], ALU.add)
        nc.scalar.activation(aa_second[:], aa[:].indirect(idx6[:, hc:]), COPY)
        nc.sync.dma_start(out[:, :half], y_first[:])
        nc.vector.tensor_tensor(y_second[:], aa_second[:], w[:, half:], ALU.add)
        nc.sync.dma_start(out[:, half:], y_second[:])
